import numpy as np
import ml_dtypes


def mxq(x, axis, fmt="e4m3"):
    dtype, down = {"e4m3": (ml_dtypes.float8_e4m3fn, 7), "e5m2": (ml_dtypes.float8_e5m2, 14)}[fmt]
    v = np.moveaxis(np.asarray(x, np.float32).astype(ml_dtypes.bfloat16).astype(np.float64), axis, -1)
    blocks = v.reshape(v.shape[:-1] + (-1, 32))
    amax = np.abs(blocks).max(-1, keepdims=True)
    byte = np.maximum(np.where(amax > 0, np.frexp(amax)[1] - 1 + 127, 0) - down, 1)
    scale = np.exp2(byte - 127.0)
    codes = (blocks / scale).astype(np.float32).astype(dtype).astype(np.float64)
    return np.moveaxis((codes * scale).reshape(v.shape), -1, axis)


WIDE = False


def mx_kscale(k):
    if not WIDE:
        return np.ones(k)
    levels = np.array([10, -10, 5, -5, 0])
    if k % 512:
        return np.exp2(np.random.permutation(np.resize(levels, k // 32))).repeat(32)
    a = np.empty((k // 512, 16))
    for p in range(k // 512):
        a[p, :8] = np.random.permutation(np.resize(levels, 8))
        for g in range(8):
            far = levels[np.abs(levels - a[p, g]) >= 10]
            a[p, g + 8] = far[np.random.randint(len(far))]
    return np.exp2(a.ravel()).repeat(32)


def f64(x):
    return np.asarray(x).astype(np.float64)


def striped(idx):
    return np.tile(idx.reshape(-1, 16).T, (8, 1)).astype(np.uint16)


def unstriped(offs):
    return offs[:16].T.reshape(-1).astype(np.int64)


E2M1 = np.array([0.0, 0.5, 1.0, 1.5, 2.0, 3.0, 4.0, 6.0, -0.0, -0.5, -1.0, -1.5, -2.0, -3.0, -4.0, -6.0])


def pack_weight(w, fmt):
    k, n = w.shape
    w = f64(np.asarray(w, np.float32).astype(ml_dtypes.bfloat16)).reshape(k // 32, 32, n)
    amax = np.abs(w).max(1)
    if fmt == "e4m3":
        byte = np.frexp(amax)[1] - 1 + 127 - 7
    else:
        mant, ex = np.frexp(amax / 6.0)
        byte = np.where(mant > 0.5, ex, ex - 1) + 127
    byte = np.clip(np.where(amax > 0, byte, 1), 1, 254)
    scaled = (w * np.exp2(127.0 - byte)[:, None, :]).reshape(k, n).astype(np.float32)
    by_word = np.ascontiguousarray(scaled.reshape(k // 512, 128, 4, n).transpose(0, 1, 3, 2))
    if fmt == "e4m3":
        words = by_word.astype(ml_dtypes.float8_e4m3fn).view(np.uint8)
    else:
        c = by_word.astype(ml_dtypes.float4_e2m1fn).view(np.uint8) & 0xF
        words = (c[..., 0::2] | (c[..., 1::2] << 4)).reshape(k // 512, 128, 2 * n)
    return np.ascontiguousarray(words), np.ascontiguousarray(byte.astype(np.uint8).reshape(k // 512, 16, n))


def unpack_weight(words, scales, fmt):
    g, _, n = scales.shape
    words = np.ascontiguousarray(words).reshape(g, 128, n, -1)
    if fmt == "e4m3":
        vals = words.view(ml_dtypes.float8_e4m3fn).astype(np.float64)
    else:
        nib = np.empty((g, 128, n, 4), np.uint8)
        nib[..., 0::2] = words & 0xF
        nib[..., 1::2] = words >> 4
        vals = E2M1[nib]
    vals = vals * np.repeat(np.exp2(scales.astype(np.float64) - 127.0), 8, axis=1)[..., None]
    return vals.transpose(0, 1, 3, 2).reshape(g * 512, n)


def gelu(v):
    return 0.5 * v * (1.0 + np.tanh(np.sqrt(2.0 / np.pi) * (v + 0.044715 * v**3)))


def bf(x):
    return np.asarray(x, np.float32).astype(ml_dtypes.bfloat16)


def planes(Y):
    n, m = Y.shape
    b = f64(bf(Y)).reshape(n // 32, 32, m)
    amax = np.abs(b).max(1)
    byte = np.clip(np.where(amax > 0, np.frexp(amax)[1] - 1 + 127 - 7, 1), 1, 254)
    codes = (b * np.exp2(127.0 - byte)[:, None, :]).reshape(n, m).astype(np.float32).astype(ml_dtypes.float8_e4m3fn).view(np.uint8)
    words = codes.reshape(n // 512, 128, 4, m).transpose(0, 1, 3, 2)
    return np.ascontiguousarray(words), np.ascontiguousarray(byte.astype(np.uint8).reshape(n // 512, 16, m))


K, K2, H, N, T, S = 1024, 512, 1024, 512, 4096, 1024

def setup_inputs():
    n = np.random.standard_normal
    s = mx_kscale(K)[:, None]
    s2 = mx_kscale(K2)[:, None]
    u = mx_kscale(H)[:, None]
    d = {}
    d["tab_words"], d["tab_scales"] = pack_weight(n((K, T)) * s, "e4m3")
    d["offs"] = striped(np.random.permutation(T)[:S])
    d["xs_words"], d["xs_scales"] = pack_weight(n((K2, S)) * s2, "e4m3")
    d["w1"] = (n((K, H)) / s * u.T / K ** 0.5).astype(np.float32)
    d["w2_words"], d["w2_scales"] = pack_weight(n((K2, H)) / s2 * u.T / K2 ** 0.5, "e2m1")
    gain = np.exp(0.8 * n(N))[None, :]
    d["w4_words"], d["w4_scales"] = pack_weight(n((H, N)) / u * gain / H ** 0.5, "e4m3")
    return d

def reference(tab_words, tab_scales, offs, xs_words, xs_scales, w1, w2_words, w2_scales, w4_words, w4_scales):
    v = unpack_weight(tab_words, tab_scales, "e4m3")[:, unstriped(offs)]
    xs = unpack_weight(xs_words, xs_scales, "e4m3")
    w2 = unpack_weight(w2_words, w2_scales, "e2m1")
    w4 = unpack_weight(w4_words, w4_scales, "e4m3")
    a = mxq(f64(w1), 0, "e4m3").T @ v
    b = w2.T @ xs
    z = np.abs(a + b) - np.abs(a - b)
    y = w4.T @ mxq(z, 0, "e4m3")
    words, scales = planes(y)
    return y, words, scales

@@ -1,0 +1,276 @@
+from contextlib import ExitStack
+
+import concourse.mybir as mybir
+
+K, K2, H, N, T, S = 1024, 512, 1024, 512, 4096, 1024
+FLOPS = 2 * S * (K * H + K2 * H + H * N)
+
+F32 = mybir.dt.float32
+BF16 = mybir.dt.bfloat16
+I32 = mybir.dt.int32
+U32 = mybir.dt.uint32
+U16 = mybir.dt.uint16
+U8 = mybir.dt.uint8
+FP8X4 = mybir.dt.float8_e4m3fn_x4
+FP4X4 = mybir.dt.float4_e2m1fn_x4
+ALU = mybir.AluOpType
+ACT = mybir.ActivationFunctionType
+
+P = 128
+PACK = 4
+KP = P * PACK
+CH = 128
+CHUNKS = S // CH
+BLOCKS = H // KP
+PASSES = K // KP
+HALF = S // 2
+SUMMED_IN_PSUM = 6
+
+
+def load_scale_rows(engine, plane, scales):
+    passes = scales.shape[0]
+    for q in range(4):
+        rows = scales[:, 4 * q : 4 * q + 4, :] if passes > 1 else scales[0, 4 * q : 4 * q + 4, :]
+        engine.dma_start(out=plane[32 * q : 32 * q + 4 * passes, :].bitcast(I32), in_=rows.bitcast(I32))
+
+
+def words_of(dram):
+    return dram.rearrange("p c i -> p (c i)").bitcast(I32)
+
+
+def tile_list_disc_parity_agreement_kernel(
+    tc, tab_words, tab_scales, offs, xs_words, xs_scales, w1, w2_words, w2_scales, w4_words, w4_scales,
+    out_0, out_1, out_2,
+):
+    nc = tc.nc
+    with ExitStack() as ctx:
+        keep = ctx.enter_context(tc.tile_pool(name="keep", bufs=1))
+        stage = ctx.enter_context(tc.tile_pool(name="stage", bufs=2))
+        ring = ctx.enter_context(tc.tile_pool(name="ring", bufs=3))
+        psum = ctx.enter_context(tc.psum_pool(name="psum", bufs=1))
+
+        def held(shape, dtype, name, tag=None):
+            return keep.tile(shape, dtype, name=name, tag=tag or name, align_bytes=64)
+
+        offsets = keep.tile([P, S // 16], U16, name="offsets")
+        w2_raw = held([P, 2 * H], U8, "w2_raw", "raw_weight")
+        w2_plane_raw = held([P, H], U8, "w2_plane_raw")
+        xs_codes = held([P, S], I32, "xs_codes")
+        xs_plane = held([P, S], U8, "xs_plane")
+        tab_plane = held([P, T], U8, "tab_plane")
+        w4_plane_raw = held([P, N], U8, "w4_plane_raw")
+        tab_codes = [held([P, T], I32, "tab_codes%d" % a) for a in range(PASSES)]
+
+        nc.gpsimd.memset(w2_plane_raw[:].bitcast(I32), 0)
+        nc.gpsimd.memset(xs_plane[:].bitcast(I32), 0)
+        nc.vector.memset(tab_plane[:].bitcast(I32), 0)
+        nc.vector.memset(w4_plane_raw[:].bitcast(I32), 0)
+
+        nc.sync.dma_start(offsets[:], offs)
+        nc.sync.dma_start(out=w2_raw[:].bitcast(I32), in_=w2_words[0].bitcast(I32))
+        load_scale_rows(nc.sync, w2_plane_raw, w2_scales)
+        nc.sync.dma_start(out=xs_codes[:], in_=words_of(xs_words[0]))
+
+        w1_codes = {}
+        w1_plane = {}
+
+        def load_w1(a, blk):
+            raw = stage.tile([P, PACK, KP], F32, name="w1_raw")
+            rows = w1[a * KP : (a + 1) * KP, blk * KP : (blk + 1) * KP]
+            nc.sync.dma_start(out=raw[:], in_=rows.rearrange("(p i) c -> p i c", i=PACK))
+            return raw
+
+        def quantize_w1(a, blk, raw, copy):
+            rounded = stage.tile([P, PACK * KP], BF16, name="w1_rounded", align_bytes=64)
+            copy(
+                out=rounded[:].rearrange("p (t m i) -> p m t i", t=PACK, i=PACK),
+                in_=raw[:].rearrange("p i (m t) -> p m t i", t=PACK),
+            )
+            w1_codes[a, blk] = held([P, KP], I32, "w1_codes%d%d" % (a, blk))
+            w1_plane[a, blk] = held([P, KP], U8, "w1_plane%d%d" % (a, blk))
+            nc.vector.quantize_mx(out=w1_codes[a, blk][:].bitcast(FP8X4), scales=w1_plane[a, blk][:], in_=rounded[:])
+
+        w1_first = [load_w1(0, 0)]
+        load_scale_rows(nc.sync, xs_plane, xs_scales)
+        w1_first.append(load_w1(1, 0))
+        load_scale_rows(nc.sync, tab_plane, tab_scales)
+        for a in range(PASSES):
+            nc.sync.dma_start(out=tab_codes[a][:], in_=words_of(tab_words[a]))
+
+        w2_codes = [held([P, 2 * KP], U8, "w2_codes%d" % blk) for blk in range(BLOCKS)]
+        w2_plane = held([P, H], U8, "w2_plane")
+        nc.vector.tensor_copy(
+            out=w2_plane[:].rearrange("p (b t m) -> p b t m", b=BLOCKS, t=PACK),
+            in_=w2_plane_raw[:].rearrange("p (b m t) -> p b t m", b=BLOCKS, t=PACK),
+        )
+        for blk in range(BLOCKS):
+            nc.vector.tensor_copy(
+                out=w2_codes[blk][:].rearrange("p (t m e) -> p t m e", t=PACK, e=2),
+                in_=w2_raw[:, blk * 2 * KP : (blk + 1) * 2 * KP].rearrange("p (m t e) -> p t m e", t=PACK, e=2),
+            )
+
+        def b_pass(bank, blk, ch, t, start, stop):
+            cols = slice(ch * CH, (ch + 1) * CH)
+            nc.tensor.matmul_mx(
+                out=bank[:, t, :],
+                lhsT=w2_codes[blk][:, t * 2 * P : (t + 1) * 2 * P].bitcast(FP4X4),
+                lhsT_scale=w2_plane[:, blk * KP + t * P : blk * KP + (t + 1) * P],
+                rhs=xs_codes[:, cols].bitcast(FP8X4),
+                rhs_scale=xs_plane[:, cols],
+                start=start,
+                stop=stop,
+            )
+
+        order = [(0, ch) for ch in range(CHUNKS // 2)]
+        for ch in range(CHUNKS // 2):
+            order.extend([(1, ch), (0, ch + CHUNKS // 2)])
+        order.extend([(1, ch) for ch in range(CHUNKS // 2, CHUNKS)])
+        units = len(order)
+        in_psum = [(i * SUMMED_IN_PSUM) // units != ((i + 1) * SUMMED_IN_PSUM) // units for i in range(units)]
+
+        def woven(bank):
+            return bank[:].rearrange("p t c -> p c t")
+
+        def as_woven(ap):
+            return ap.rearrange("p (c t) -> p c t", t=PACK)
+
+        b_sb = []
+        for i, (blk, ch) in enumerate(order):
+            bank = psum.tile([P, PACK, CH], F32, name="side", bufs=3)
+            for t in range(PACK):
+                b_pass(bank, blk, ch, t, True, True)
+            b_sb.append(held([P, KP], F32, "b_sb%d" % i))
+            nc.scalar.activation(out=as_woven(b_sb[i][:]), in_=woven(bank), func=ACT.Copy, scale=2.0 if in_psum[i] else 1.0)
+
+        for a in range(PASSES):
+            quantize_w1(a, 0, w1_first[a], nc.vector.tensor_copy)
+
+        v_plane = held([P, S], U8, "v_plane")
+        nc.vector.tensor_copy(out=v_plane[:], in_=tab_plane[:].indirect(offsets[:]))
+        v_codes = {}
+        for a in range(PASSES):
+            for h in range(2):
+                v_codes[a, h] = held([P, HALF], I32, "v_codes%d%d" % (a, h))
+                nc.vector.tensor_copy(
+                    out=v_codes[a, h][:].bitcast(U32),
+                    in_=tab_codes[a][:].bitcast(U32).indirect(offsets[:, h * HALF // 16 : (h + 1) * HALF // 16]),
+                )
+
+        w1_second = [load_w1(a, 1) for a in range(PASSES)]
+        w4_raw = held([P, BLOCKS * N], I32, "w4_raw", "raw_weight")
+        nc.sync.dma_start(
+            out=w4_raw[:].rearrange("p (b c) -> p b c", b=BLOCKS),
+            in_=w4_words.rearrange("b p c i -> p b (c i)").bitcast(I32),
+        )
+        load_scale_rows(nc.sync, w4_plane_raw, w4_scales)
+        w4_codes = held([P, BLOCKS * N], I32, "w4_codes")
+        w4_plane = held([P, N], U8, "w4_plane")
+
+        z_codes = [held([P, S], I32, "z_codes%d" % blk) for blk in range(BLOCKS)]
+        z_plane = [held([P, S], U8, "z_plane%d" % blk) for blk in range(BLOCKS)]
+        y_codes = held([P, S], I32, "y_codes")
+        y_plane = held([P, S], U8, "y_plane")
+        y_rows = out_0.rearrange("(p t) j -> p t j", t=PACK)
+        y_words = words_of(out_1[0])
+
+        magnitudes = {}
+        z_rounded = {}
+        y_rounded = {}
+
+        def first_stage(i):
+            blk, ch = order[i]
+            h, c0 = divmod(ch * CH, HALF)
+            bank = psum.tile([P, PACK, CH], F32, name="acc", bufs=5)
+            for a in range(PASSES):
+                for t in range(PACK):
+                    nc.tensor.matmul_mx(
+                        out=bank[:, t, :],
+                        lhsT=w1_codes[a, blk][:, t * P : (t + 1) * P].bitcast(FP8X4),
+                        lhsT_scale=w1_plane[a, blk][:, t * P : (t + 1) * P],
+                        rhs=v_codes[a, h][:, c0 : c0 + CH].bitcast(FP8X4),
+                        rhs_scale=v_plane[4 * a :, ch * CH : (ch + 1) * CH],
+                        start=(a == 0 and t == 0),
+                        stop=(a == PASSES - 1 and t == PACK - 1 and not in_psum[i]),
+                    )
+            diff = ring.tile([P, KP], F32, name="diff")
+            abs_sum = ring.tile([P, KP], F32, name="abs_sum")
+            abs_diff = ring.tile([P, KP], F32, name="abs_diff")
+            if in_psum[i]:
+                for t in range(PACK):
+                    b_pass(bank, blk, ch, t, False, t == PACK - 1)
+                nc.vector.tensor_tensor(out=as_woven(diff[:]), in0=woven(bank), in1=as_woven(b_sb[i][:]), op=ALU.subtract)
+                nc.scalar.activation(out=as_woven(abs_sum[:]), in_=woven(bank), func=ACT.Abs)
+            else:
+                total = ring.tile([P, KP], F32, name="total")
+                nc.vector.tensor_tensor(out=as_woven(total[:]), in0=woven(bank), in1=as_woven(b_sb[i][:]), op=ALU.add)
+                nc.vector.tensor_tensor(out=as_woven(diff[:]), in0=woven(bank), in1=as_woven(b_sb[i][:]), op=ALU.subtract)
+                nc.scalar.activation(out=abs_sum[:], in_=total[:], func=ACT.Abs)
+            nc.scalar.activation(out=abs_diff[:], in_=diff[:], func=ACT.Abs)
+            magnitudes[i] = (abs_sum, abs_diff)
+
+        def agree(i):
+            z_rounded[i] = ring.tile([P, KP], BF16, name="z_rounded", align_bytes=64)
+            nc.vector.tensor_tensor(out=z_rounded[i][:], in0=magnitudes[i][0][:], in1=magnitudes[i][1][:], op=ALU.subtract)
+
+        def quantize_z(i):
+            blk, ch = order[i]
+            cols = slice(ch * CH, (ch + 1) * CH)
+            nc.vector.quantize_mx(out=z_codes[blk][:, cols].bitcast(FP8X4), scales=z_plane[blk][:, cols], in_=z_rounded[i][:])
+
+        def second_stage(ch):
+            cols = slice(ch * CH, (ch + 1) * CH)
+            bank = psum.tile([P, PACK, CH], F32, name="side", bufs=3)
+            for blk in range(BLOCKS):
+                for t in range(PACK):
+                    nc.tensor.matmul_mx(
+                        out=bank[:, t, :],
+                        lhsT=w4_codes[:, blk * N + t * P : blk * N + (t + 1) * P].bitcast(FP8X4),
+                        lhsT_scale=w4_plane[4 * blk :, t * P : (t + 1) * P],
+                        rhs=z_codes[blk][:, cols].bitcast(FP8X4),
+                        rhs_scale=z_plane[blk][:, cols],
+                        start=(blk == 0 and t == 0),
+                        stop=(blk == BLOCKS - 1 and t == PACK - 1),
+                    )
+            y = ring.tile([P, PACK, CH], F32, name="y")
+            nc.scalar.copy(out=y[:], in_=bank[:])
+            nc.sync.dma_start(out=y_rows[:, :, cols], in_=y[:])
+            y_rounded[ch] = ring.tile([P, KP], BF16, name="y_rounded", align_bytes=64)
+            if ch < CHUNKS // 2:
+                nc.scalar.copy(out=as_woven(y_rounded[ch][:]), in_=woven(bank))
+            else:
+                nc.vector.tensor_copy(out=as_woven(y_rounded[ch][:]), in_=woven(y))
+
+        def quantize_y(ch):
+            cols = slice(ch * CH, (ch + 1) * CH)
+            nc.vector.quantize_mx(out=y_codes[:, cols].bitcast(FP8X4), scales=y_plane[:, cols], in_=y_rounded[ch][:])
+            nc.sync.dma_start(out=y_words[:, cols], in_=y_codes[:, cols])
+
+        for step in range(units + 4):
+            if step < units:
+                first_stage(step)
+            if step < PASSES:
+                quantize_w1(step, 1, w1_second[step], nc.scalar.copy)
+            if step == PASSES:
+                nc.vector.tensor_copy(
+                    out=w4_codes[:].rearrange("p (b t m) -> p b t m", b=BLOCKS, t=PACK),
+                    in_=w4_raw[:].rearrange("p (b m t) -> p b t m", b=BLOCKS, t=PACK),
+                )
+                nc.vector.tensor_copy(
+                    out=w4_plane[:].rearrange("p (t m) -> p t m", t=PACK),
+                    in_=w4_plane_raw[:].rearrange("p (m t) -> p t m", t=PACK),
+                )
+            if 0 <= step - 1 < units:
+                agree(step - 1)
+            if 0 <= step - 2 < units:
+                quantize_z(step - 2)
+                if order[step - 2][0] == BLOCKS - 1:
+                    second_stage(order[step - 2][1])
+            if 0 <= step - 4 < units and order[step - 4][0] == BLOCKS - 1:
+                quantize_y(order[step - 4][1])
+
+        for q in range(4):
+            engine = nc.sync if q % 2 == 0 else nc.scalar
+            engine.dma_start(
+                out=out_2[0, 4 * q : 4 * q + 4, :].bitcast(I32),
+                in_=y_plane[32 * q : 32 * q + 4, :].bitcast(I32),
+            )

@@ -25,6 +25,7 @@ BLOCKS = H // KP
 PASSES = K // KP
 HALF = S // 2
 SUMMED_IN_PSUM = 6
+ROUNDED_ON_VECTOR = 3
 
 
 def load_scale_rows(engine, plane, scales):
@@ -32,6 +33,12 @@ def load_scale_rows(engine, plane, scales):
     for q in range(4):
         rows = scales[:, 4 * q : 4 * q + 4, :] if passes > 1 else scales[0, 4 * q : 4 * q + 4, :]
         engine.dma_start(out=plane[32 * q : 32 * q + 4 * passes, :].bitcast(I32), in_=rows.bitcast(I32))
+
+
+def load_pass_rows(engine, plane, scales, a):
+    for q in range(4):
+        first = 32 * q + 4 * a
+        engine.dma_start(out=plane[first : first + 4, :].bitcast(I32), in_=scales[a, 4 * q : 4 * q + 4, :].bitcast(I32))
 
 
 def words_of(dram):
@@ -46,7 +53,7 @@ def tile_list_disc_parity_agreement_kernel(
     with ExitStack() as ctx:
         keep = ctx.enter_context(tc.tile_pool(name="keep", bufs=1))
         stage = ctx.enter_context(tc.tile_pool(name="stage", bufs=2))
-        ring = ctx.enter_context(tc.tile_pool(name="ring", bufs=3))
+        ring = ctx.enter_context(tc.tile_pool(name="ring", bufs=4))
         psum = ctx.enter_context(tc.psum_pool(name="psum", bufs=1))
 
         def held(shape, dtype, name, tag=None):
@@ -82,20 +89,22 @@ def tile_list_disc_parity_agreement_kernel(
 
         def quantize_w1(a, blk, raw, copy):
             rounded = stage.tile([P, PACK * KP], BF16, name="w1_rounded", align_bytes=64)
-            copy(
-                out=rounded[:].rearrange("p (t m i) -> p m t i", t=PACK, i=PACK),
-                in_=raw[:].rearrange("p i (m t) -> p m t i", t=PACK),
-            )
+            for m0 in range(0, P, P // 2):
+                copy(
+                    out=rounded[:].rearrange("p (t m i) -> p m i t", t=PACK, i=PACK)[:, m0 : m0 + P // 2],
+                    in_=raw[:].rearrange("p i (m t) -> p m i t", t=PACK)[:, m0 : m0 + P // 2],
+                )
             w1_codes[a, blk] = held([P, KP], I32, "w1_codes%d%d" % (a, blk))
             w1_plane[a, blk] = held([P, KP], U8, "w1_plane%d%d" % (a, blk))
             nc.vector.quantize_mx(out=w1_codes[a, blk][:].bitcast(FP8X4), scales=w1_plane[a, blk][:], in_=rounded[:])
 
         w1_first = [load_w1(0, 0)]
         load_scale_rows(nc.sync, xs_plane, xs_scales)
+        nc.sync.dma_start(out=tab_codes[0][:], in_=words_of(tab_words[0]))
+        load_pass_rows(nc.sync, tab_plane, tab_scales, 0)
         w1_first.append(load_w1(1, 0))
-        load_scale_rows(nc.sync, tab_plane, tab_scales)
-        for a in range(PASSES):
-            nc.sync.dma_start(out=tab_codes[a][:], in_=words_of(tab_words[a]))
+        load_pass_rows(nc.sync, tab_plane, tab_scales, 1)
+        nc.sync.dma_start(out=tab_codes[1][:], in_=words_of(tab_words[1]))
 
         w2_codes = [held([P, 2 * KP], U8, "w2_codes%d" % blk) for blk in range(BLOCKS)]
         w2_plane = held([P, H], U8, "w2_plane")
@@ -126,7 +135,7 @@ def tile_list_disc_parity_agreement_kernel(
             order.extend([(1, ch), (0, ch + CHUNKS // 2)])
         order.extend([(1, ch) for ch in range(CHUNKS // 2, CHUNKS)])
         units = len(order)
-        in_psum = [(i * SUMMED_IN_PSUM) // units != ((i + 1) * SUMMED_IN_PSUM) // units for i in range(units)]
+        in_psum = [i >= units - SUMMED_IN_PSUM for i in range(units)]
 
         def woven(bank):
             return bank[:].rearrange("p t c -> p c t")
@@ -142,19 +151,22 @@ def tile_list_disc_parity_agreement_kernel(
             b_sb.append(held([P, KP], F32, "b_sb%d" % i))
             nc.scalar.activation(out=as_woven(b_sb[i][:]), in_=woven(bank), func=ACT.Copy, scale=2.0 if in_psum[i] else 1.0)
 
-        for a in range(PASSES):
-            quantize_w1(a, 0, w1_first[a], nc.vector.tensor_copy)
-
         v_plane = held([P, S], U8, "v_plane")
-        nc.vector.tensor_copy(out=v_plane[:], in_=tab_plane[:].indirect(offsets[:]))
         v_codes = {}
-        for a in range(PASSES):
+
+        def gather_words(a):
             for h in range(2):
                 v_codes[a, h] = held([P, HALF], I32, "v_codes%d%d" % (a, h))
                 nc.vector.tensor_copy(
                     out=v_codes[a, h][:].bitcast(U32),
                     in_=tab_codes[a][:].bitcast(U32).indirect(offsets[:, h * HALF // 16 : (h + 1) * HALF // 16]),
                 )
+
+        quantize_w1(0, 0, w1_first[0], nc.vector.tensor_copy)
+        gather_words(0)
+        quantize_w1(1, 0, w1_first[1], nc.vector.tensor_copy)
+        nc.vector.tensor_copy(out=v_plane[:], in_=tab_plane[:].indirect(offsets[:]))
+        gather_words(1)
 
         w1_second = [load_w1(a, 1) for a in range(PASSES)]
         w4_raw = held([P, BLOCKS * N], I32, "w4_raw", "raw_weight")
@@ -235,17 +247,20 @@ def tile_list_disc_parity_agreement_kernel(
             nc.scalar.copy(out=y[:], in_=bank[:])
             nc.sync.dma_start(out=y_rows[:, :, cols], in_=y[:])
             y_rounded[ch] = ring.tile([P, KP], BF16, name="y_rounded", align_bytes=64)
-            if ch < CHUNKS // 2:
+            if ch < CHUNKS - ROUNDED_ON_VECTOR:
                 nc.scalar.copy(out=as_woven(y_rounded[ch][:]), in_=woven(bank))
             else:
-                nc.vector.tensor_copy(out=as_woven(y_rounded[ch][:]), in_=woven(y))
+                nc.vector.tensor_copy(
+                    out=y_rounded[ch][:].rearrange("p (c i t) -> p c t i", i=PACK, t=PACK),
+                    in_=y[:].rearrange("p t (c i) -> p c t i", i=PACK),
+                )
 
         def quantize_y(ch):
             cols = slice(ch * CH, (ch + 1) * CH)
             nc.vector.quantize_mx(out=y_codes[:, cols].bitcast(FP8X4), scales=y_plane[:, cols], in_=y_rounded[ch][:])
             nc.sync.dma_start(out=y_words[:, cols], in_=y_codes[:, cols])
 
-        for step in range(units + 4):
+        for step in range(units + 5):
             if step < units:
                 first_stage(step)
             if step < PASSES:
@@ -259,14 +274,14 @@ def tile_list_disc_parity_agreement_kernel(
                     out=w4_plane[:].rearrange("p (t m) -> p t m", t=PACK),
                     in_=w4_plane_raw[:].rearrange("p (m t) -> p t m", t=PACK),
                 )
-            if 0 <= step - 1 < units:
-                agree(step - 1)
             if 0 <= step - 2 < units:
-                quantize_z(step - 2)
-                if order[step - 2][0] == BLOCKS - 1:
-                    second_stage(order[step - 2][1])
-            if 0 <= step - 4 < units and order[step - 4][0] == BLOCKS - 1:
-                quantize_y(order[step - 4][1])
+                agree(step - 2)
+            if 0 <= step - 3 < units:
+                quantize_z(step - 3)
+                if order[step - 3][0] == BLOCKS - 1:
+                    second_stage(order[step - 3][1])
+            if 0 <= step - 5 < units and order[step - 5][0] == BLOCKS - 1:
+                quantize_y(order[step - 5][1])
 
         for q in range(4):
             engine = nc.sync if q % 2 == 0 else nc.scalar

@@ -25,7 +25,7 @@ BLOCKS = H // KP
 PASSES = K // KP
 HALF = S // 2
 SUMMED_IN_PSUM = 6
-ROUNDED_ON_VECTOR = 3
+ROUNDED_ON_VECTOR = 8
 
 
 def load_scale_rows(engine, plane, scales):
@@ -135,7 +135,7 @@ def tile_list_disc_parity_agreement_kernel(
             order.extend([(1, ch), (0, ch + CHUNKS // 2)])
         order.extend([(1, ch) for ch in range(CHUNKS // 2, CHUNKS)])
         units = len(order)
-        in_psum = [i >= units - SUMMED_IN_PSUM for i in range(units)]
+        in_psum = [i % 2 == 1 and i >= units - 2 * SUMMED_IN_PSUM for i in range(units)]
 
         def woven(bank):
             return bank[:].rearrange("p t c -> p c t")
@@ -188,6 +188,7 @@ def tile_list_disc_parity_agreement_kernel(
         magnitudes = {}
         z_rounded = {}
         y_rounded = {}
+        y_sums = {}
 
         def first_stage(i):
             blk, ch = order[i]
@@ -221,13 +222,16 @@ def tile_list_disc_parity_agreement_kernel(
             magnitudes[i] = (abs_sum, abs_diff)
 
         def agree(i):
-            z_rounded[i] = ring.tile([P, KP], BF16, name="z_rounded", align_bytes=64)
-            nc.vector.tensor_tensor(out=z_rounded[i][:], in0=magnitudes[i][0][:], in1=magnitudes[i][1][:], op=ALU.subtract)
+            if i % 2 == 0:
+                pair = held([P, 2 * KP], BF16, "z_pair")
+                z_rounded[i], z_rounded[i + 1] = pair[:, :KP], pair[:, KP:]
+            engine = nc.gpsimd if i % 2 == 0 else nc.vector
+            engine.tensor_tensor(out=z_rounded[i], in0=magnitudes[i][0][:], in1=magnitudes[i][1][:], op=ALU.subtract)
 
         def quantize_z(i):
             blk, ch = order[i]
             cols = slice(ch * CH, (ch + 1) * CH)
-            nc.vector.quantize_mx(out=z_codes[blk][:, cols].bitcast(FP8X4), scales=z_plane[blk][:, cols], in_=z_rounded[i][:])
+            nc.vector.quantize_mx(out=z_codes[blk][:, cols].bitcast(FP8X4), scales=z_plane[blk][:, cols], in_=z_rounded[i])
 
         def second_stage(ch):
             cols = slice(ch * CH, (ch + 1) * CH)
@@ -246,6 +250,10 @@ def tile_list_disc_parity_agreement_kernel(
             y = ring.tile([P, PACK, CH], F32, name="y")
             nc.scalar.copy(out=y[:], in_=bank[:])
             nc.sync.dma_start(out=y_rows[:, :, cols], in_=y[:])
+            y_sums[ch] = (bank, y)
+
+        def round_y(ch):
+            bank, y = y_sums[ch]
             y_rounded[ch] = ring.tile([P, KP], BF16, name="y_rounded", align_bytes=64)
             if ch < CHUNKS - ROUNDED_ON_VECTOR:
                 nc.scalar.copy(out=as_woven(y_rounded[ch][:]), in_=woven(bank))
@@ -260,12 +268,20 @@ def tile_list_disc_parity_agreement_kernel(
             nc.vector.quantize_mx(out=y_codes[:, cols].bitcast(FP8X4), scales=y_plane[:, cols], in_=y_rounded[ch][:])
             nc.sync.dma_start(out=y_words[:, cols], in_=y_codes[:, cols])
 
-        for step in range(units + 5):
-            if step < units:
-                first_stage(step)
-            if step < PASSES:
-                quantize_w1(step, 1, w1_second[step], nc.scalar.copy)
-            if step == PASSES:
+        def closing(pair):
+            return [order[i][1] for i in (2 * pair, 2 * pair + 1) if 0 <= i < units and order[i][0] == BLOCKS - 1]
+
+        pairs = units // 2
+        for step in range(pairs + 3):
+            if 0 <= step - 1 < pairs:
+                agree(2 * step - 2)
+            if step < pairs:
+                first_stage(2 * step)
+                first_stage(2 * step + 1)
+            if step == 0:
+                for a in range(PASSES):
+                    quantize_w1(a, 1, w1_second[a], nc.scalar.copy)
+            if step == 1:
                 nc.vector.tensor_copy(
                     out=w4_codes[:].rearrange("p (b t m) -> p b t m", b=BLOCKS, t=PACK),
                     in_=w4_raw[:].rearrange("p (b m t) -> p b t m", b=BLOCKS, t=PACK),
@@ -274,14 +290,17 @@ def tile_list_disc_parity_agreement_kernel(
                     out=w4_plane[:].rearrange("p (t m) -> p t m", t=PACK),
                     in_=w4_plane_raw[:].rearrange("p (m t) -> p t m", t=PACK),
                 )
-            if 0 <= step - 2 < units:
-                agree(step - 2)
-            if 0 <= step - 3 < units:
-                quantize_z(step - 3)
-                if order[step - 3][0] == BLOCKS - 1:
-                    second_stage(order[step - 3][1])
-            if 0 <= step - 5 < units and order[step - 5][0] == BLOCKS - 1:
-                quantize_y(order[step - 5][1])
+            for ch in closing(step - 2):
+                round_y(ch)
+            if 0 <= step - 1 < pairs:
+                agree(2 * step - 1)
+            for ch in closing(step - 2):
+                quantize_y(ch)
+            if 0 <= step - 1 < pairs:
+                quantize_z(2 * step - 2)
+                quantize_z(2 * step - 1)
+            for ch in closing(step - 1):
+                second_stage(ch)
 
         for q in range(4):
             engine = nc.sync if q % 2 == 0 else nc.scalar

from contextlib import ExitStack

import concourse.mybir as mybir

K, K2, H, N, T, S = 1024, 512, 1024, 512, 4096, 1024
FLOPS = 2 * S * (K * H + K2 * H + H * N)

F32 = mybir.dt.float32
BF16 = mybir.dt.bfloat16
I32 = mybir.dt.int32
U32 = mybir.dt.uint32
U16 = mybir.dt.uint16
U8 = mybir.dt.uint8
FP8X4 = mybir.dt.float8_e4m3fn_x4
FP4X4 = mybir.dt.float4_e2m1fn_x4
ALU = mybir.AluOpType
ACT = mybir.ActivationFunctionType

P = 128
PACK = 4
KP = P * PACK
CH = 128
CHUNKS = S // CH
BLOCKS = H // KP
PASSES = K // KP
HALF = S // 2
SUMMED_IN_PSUM = 6
ROUNDED_ON_VECTOR = 8


def load_scale_rows(engine, plane, scales):
    passes = scales.shape[0]
    for q in range(4):
        rows = scales[:, 4 * q : 4 * q + 4, :] if passes > 1 else scales[0, 4 * q : 4 * q + 4, :]
        engine.dma_start(out=plane[32 * q : 32 * q + 4 * passes, :].bitcast(I32), in_=rows.bitcast(I32))


def load_pass_rows(engine, plane, scales, a):
    for q in range(4):
        first = 32 * q + 4 * a
        engine.dma_start(out=plane[first : first + 4, :].bitcast(I32), in_=scales[a, 4 * q : 4 * q + 4, :].bitcast(I32))


def words_of(dram):
    return dram.rearrange("p c i -> p (c i)").bitcast(I32)


def tile_list_disc_parity_agreement_kernel(
    tc, tab_words, tab_scales, offs, xs_words, xs_scales, w1, w2_words, w2_scales, w4_words, w4_scales,
    out_0, out_1, out_2,
):
    nc = tc.nc
    with ExitStack() as ctx:
        keep = ctx.enter_context(tc.tile_pool(name="keep", bufs=1))
        stage = ctx.enter_context(tc.tile_pool(name="stage", bufs=2))
        ring = ctx.enter_context(tc.tile_pool(name="ring", bufs=4))
        psum = ctx.enter_context(tc.psum_pool(name="psum", bufs=1))

        def held(shape, dtype, name, tag=None):
            return keep.tile(shape, dtype, name=name, tag=tag or name, align_bytes=64)

        offsets = keep.tile([P, S // 16], U16, name="offsets")
        w2_raw = held([P, 2 * H], U8, "w2_raw", "raw_weight")
        w2_plane_raw = held([P, H], U8, "w2_plane_raw")
        xs_codes = held([P, S], I32, "xs_codes")
        xs_plane = held([P, S], U8, "xs_plane")
        tab_plane = held([P, T], U8, "tab_plane")
        w4_plane_raw = held([P, N], U8, "w4_plane_raw")
        tab_codes = [held([P, T], I32, "tab_codes%d" % a) for a in range(PASSES)]

        nc.gpsimd.memset(w2_plane_raw[:].bitcast(I32), 0)
        nc.gpsimd.memset(xs_plane[:].bitcast(I32), 0)
        nc.vector.memset(tab_plane[:].bitcast(I32), 0)
        nc.vector.memset(w4_plane_raw[:].bitcast(I32), 0)

        nc.sync.dma_start(offsets[:], offs)
        nc.sync.dma_start(out=w2_raw[:].bitcast(I32), in_=w2_words[0].bitcast(I32))
        load_scale_rows(nc.sync, w2_plane_raw, w2_scales)
        nc.sync.dma_start(out=xs_codes[:], in_=words_of(xs_words[0]))

        w1_codes = {}
        w1_plane = {}

        def load_w1(a, blk):
            raw = stage.tile([P, PACK, KP], F32, name="w1_raw")
            rows = w1[a * KP : (a + 1) * KP, blk * KP : (blk + 1) * KP]
            nc.sync.dma_start(out=raw[:], in_=rows.rearrange("(p i) c -> p i c", i=PACK))
            return raw

        def quantize_w1(a, blk, raw, copy):
            rounded = stage.tile([P, PACK * KP], BF16, name="w1_rounded", align_bytes=64)
            for m0 in range(0, P, P // 2):
                copy(
                    out=rounded[:].rearrange("p (t m i) -> p m i t", t=PACK, i=PACK)[:, m0 : m0 + P // 2],
                    in_=raw[:].rearrange("p i (m t) -> p m i t", t=PACK)[:, m0 : m0 + P // 2],
                )
            w1_codes[a, blk] = held([P, KP], I32, "w1_codes%d%d" % (a, blk))
            w1_plane[a, blk] = held([P, KP], U8, "w1_plane%d%d" % (a, blk))
            nc.vector.quantize_mx(out=w1_codes[a, blk][:].bitcast(FP8X4), scales=w1_plane[a, blk][:], in_=rounded[:])

        w1_first = [load_w1(0, 0)]
        load_scale_rows(nc.sync, xs_plane, xs_scales)
        nc.sync.dma_start(out=tab_codes[0][:], in_=words_of(tab_words[0]))
        load_pass_rows(nc.sync, tab_plane, tab_scales, 0)
        w1_first.append(load_w1(1, 0))
        load_pass_rows(nc.sync, tab_plane, tab_scales, 1)
        nc.sync.dma_start(out=tab_codes[1][:], in_=words_of(tab_words[1]))

        w2_codes = [held([P, 2 * KP], U8, "w2_codes%d" % blk) for blk in range(BLOCKS)]
        w2_plane = held([P, H], U8, "w2_plane")
        nc.vector.tensor_copy(
            out=w2_plane[:].rearrange("p (b t m) -> p b t m", b=BLOCKS, t=PACK),
            in_=w2_plane_raw[:].rearrange("p (b m t) -> p b t m", b=BLOCKS, t=PACK),
        )
        for blk in range(BLOCKS):
            nc.vector.tensor_copy(
                out=w2_codes[blk][:].rearrange("p (t m e) -> p t m e", t=PACK, e=2),
                in_=w2_raw[:, blk * 2 * KP : (blk + 1) * 2 * KP].rearrange("p (m t e) -> p t m e", t=PACK, e=2),
            )

        def b_pass(bank, blk, ch, t, start, stop):
            cols = slice(ch * CH, (ch + 1) * CH)
            nc.tensor.matmul_mx(
                out=bank[:, t, :],
                lhsT=w2_codes[blk][:, t * 2 * P : (t + 1) * 2 * P].bitcast(FP4X4),
                lhsT_scale=w2_plane[:, blk * KP + t * P : blk * KP + (t + 1) * P],
                rhs=xs_codes[:, cols].bitcast(FP8X4),
                rhs_scale=xs_plane[:, cols],
                start=start,
                stop=stop,
            )

        order = [(0, ch) for ch in range(CHUNKS // 2)]
        for ch in range(CHUNKS // 2):
            order.extend([(1, ch), (0, ch + CHUNKS // 2)])
        order.extend([(1, ch) for ch in range(CHUNKS // 2, CHUNKS)])
        units = len(order)
        in_psum = [i % 2 == 1 and i >= units - 2 * SUMMED_IN_PSUM for i in range(units)]

        def woven(bank):
            return bank[:].rearrange("p t c -> p c t")

        def as_woven(ap):
            return ap.rearrange("p (c t) -> p c t", t=PACK)

        b_sb = []
        for i, (blk, ch) in enumerate(order):
            bank = psum.tile([P, PACK, CH], F32, name="side", bufs=3)
            for t in range(PACK):
                b_pass(bank, blk, ch, t, True, True)
            b_sb.append(held([P, KP], F32, "b_sb%d" % i))
            nc.scalar.activation(out=as_woven(b_sb[i][:]), in_=woven(bank), func=ACT.Copy, scale=2.0 if in_psum[i] else 1.0)

        v_plane = held([P, S], U8, "v_plane")
        v_codes = {}

        def gather_words(a):
            for h in range(2):
                v_codes[a, h] = held([P, HALF], I32, "v_codes%d%d" % (a, h))
                nc.vector.tensor_copy(
                    out=v_codes[a, h][:].bitcast(U32),
                    in_=tab_codes[a][:].bitcast(U32).indirect(offsets[:, h * HALF // 16 : (h + 1) * HALF // 16]),
                )

        quantize_w1(0, 0, w1_first[0], nc.vector.tensor_copy)
        gather_words(0)
        quantize_w1(1, 0, w1_first[1], nc.vector.tensor_copy)
        nc.vector.tensor_copy(out=v_plane[:], in_=tab_plane[:].indirect(offsets[:]))
        gather_words(1)

        w1_second = [load_w1(a, 1) for a in range(PASSES)]
        w4_raw = held([P, BLOCKS * N], I32, "w4_raw", "raw_weight")
        nc.sync.dma_start(
            out=w4_raw[:].rearrange("p (b c) -> p b c", b=BLOCKS),
            in_=w4_words.rearrange("b p c i -> p b (c i)").bitcast(I32),
        )
        load_scale_rows(nc.sync, w4_plane_raw, w4_scales)
        w4_codes = held([P, BLOCKS * N], I32, "w4_codes")
        w4_plane = held([P, N], U8, "w4_plane")

        z_codes = [held([P, S], I32, "z_codes%d" % blk) for blk in range(BLOCKS)]
        z_plane = [held([P, S], U8, "z_plane%d" % blk) for blk in range(BLOCKS)]
        y_codes = held([P, S], I32, "y_codes")
        y_plane = held([P, S], U8, "y_plane")
        y_rows = out_0.rearrange("(p t) j -> p t j", t=PACK)
        y_words = words_of(out_1[0])

        magnitudes = {}
        z_rounded = {}
        y_rounded = {}
        y_sums = {}

        def first_stage(i):
            blk, ch = order[i]
            h, c0 = divmod(ch * CH, HALF)
            bank = psum.tile([P, PACK, CH], F32, name="acc", bufs=5)
            for a in range(PASSES):
                for t in range(PACK):
                    nc.tensor.matmul_mx(
                        out=bank[:, t, :],
                        lhsT=w1_codes[a, blk][:, t * P : (t + 1) * P].bitcast(FP8X4),
                        lhsT_scale=w1_plane[a, blk][:, t * P : (t + 1) * P],
                        rhs=v_codes[a, h][:, c0 : c0 + CH].bitcast(FP8X4),
                        rhs_scale=v_plane[4 * a :, ch * CH : (ch + 1) * CH],
                        start=(a == 0 and t == 0),
                        stop=(a == PASSES - 1 and t == PACK - 1 and not in_psum[i]),
                    )
            diff = ring.tile([P, KP], F32, name="diff")
            abs_sum = ring.tile([P, KP], F32, name="abs_sum")
            abs_diff = ring.tile([P, KP], F32, name="abs_diff")
            if in_psum[i]:
                for t in range(PACK):
                    b_pass(bank, blk, ch, t, False, t == PACK - 1)
                nc.vector.tensor_tensor(out=as_woven(diff[:]), in0=woven(bank), in1=as_woven(b_sb[i][:]), op=ALU.subtract)
                nc.scalar.activation(out=as_woven(abs_sum[:]), in_=woven(bank), func=ACT.Abs)
            else:
                total = ring.tile([P, KP], F32, name="total")
                nc.vector.tensor_tensor(out=as_woven(total[:]), in0=woven(bank), in1=as_woven(b_sb[i][:]), op=ALU.add)
                nc.vector.tensor_tensor(out=as_woven(diff[:]), in0=woven(bank), in1=as_woven(b_sb[i][:]), op=ALU.subtract)
                nc.scalar.activation(out=abs_sum[:], in_=total[:], func=ACT.Abs)
            nc.scalar.activation(out=abs_diff[:], in_=diff[:], func=ACT.Abs)
            magnitudes[i] = (abs_sum, abs_diff)

        def agree(i):
            if i % 2 == 0:
                pair = held([P, 2 * KP], BF16, "z_pair")
                z_rounded[i], z_rounded[i + 1] = pair[:, :KP], pair[:, KP:]
            engine = nc.gpsimd if i % 2 == 0 else nc.vector
            engine.tensor_tensor(out=z_rounded[i], in0=magnitudes[i][0][:], in1=magnitudes[i][1][:], op=ALU.subtract)

        def quantize_z(i):
            blk, ch = order[i]
            cols = slice(ch * CH, (ch + 1) * CH)
            nc.vector.quantize_mx(out=z_codes[blk][:, cols].bitcast(FP8X4), scales=z_plane[blk][:, cols], in_=z_rounded[i])

        def second_stage(ch):
            cols = slice(ch * CH, (ch + 1) * CH)
            bank = psum.tile([P, PACK, CH], F32, name="side", bufs=3)
            for blk in range(BLOCKS):
                for t in range(PACK):
                    nc.tensor.matmul_mx(
                        out=bank[:, t, :],
                        lhsT=w4_codes[:, blk * N + t * P : blk * N + (t + 1) * P].bitcast(FP8X4),
                        lhsT_scale=w4_plane[4 * blk :, t * P : (t + 1) * P],
                        rhs=z_codes[blk][:, cols].bitcast(FP8X4),
                        rhs_scale=z_plane[blk][:, cols],
                        start=(blk == 0 and t == 0),
                        stop=(blk == BLOCKS - 1 and t == PACK - 1),
                    )
            y = ring.tile([P, PACK, CH], F32, name="y")
            nc.scalar.copy(out=y[:], in_=bank[:])
            nc.sync.dma_start(out=y_rows[:, :, cols], in_=y[:])
            y_sums[ch] = (bank, y)

        def round_y(ch):
            bank, y = y_sums[ch]
            y_rounded[ch] = ring.tile([P, KP], BF16, name="y_rounded", align_bytes=64)
            if ch < CHUNKS - ROUNDED_ON_VECTOR:
                nc.scalar.copy(out=as_woven(y_rounded[ch][:]), in_=woven(bank))
            else:
                nc.vector.tensor_copy(
                    out=y_rounded[ch][:].rearrange("p (c i t) -> p c t i", i=PACK, t=PACK),
                    in_=y[:].rearrange("p t (c i) -> p c t i", i=PACK),
                )

        def quantize_y(ch):
            cols = slice(ch * CH, (ch + 1) * CH)
            nc.vector.quantize_mx(out=y_codes[:, cols].bitcast(FP8X4), scales=y_plane[:, cols], in_=y_rounded[ch][:])
            nc.sync.dma_start(out=y_words[:, cols], in_=y_codes[:, cols])

        def closing(pair):
            return [order[i][1] for i in (2 * pair, 2 * pair + 1) if 0 <= i < units and order[i][0] == BLOCKS - 1]

        pairs = units // 2
        for step in range(pairs + 3):
            if 0 <= step - 1 < pairs:
                agree(2 * step - 2)
            if step < pairs:
                first_stage(2 * step)
                first_stage(2 * step + 1)
            if step == 0:
                for a in range(PASSES):
                    quantize_w1(a, 1, w1_second[a], nc.scalar.copy)
            if step == 1:
                nc.vector.tensor_copy(
                    out=w4_codes[:].rearrange("p (b t m) -> p b t m", b=BLOCKS, t=PACK),
                    in_=w4_raw[:].rearrange("p (b m t) -> p b t m", b=BLOCKS, t=PACK),
                )
                nc.vector.tensor_copy(
                    out=w4_plane[:].rearrange("p (t m) -> p t m", t=PACK),
                    in_=w4_plane_raw[:].rearrange("p (m t) -> p t m", t=PACK),
                )
            for ch in closing(step - 2):
                round_y(ch)
            if 0 <= step - 1 < pairs:
                agree(2 * step - 1)
            for ch in closing(step - 2):
                quantize_y(ch)
            if 0 <= step - 1 < pairs:
                quantize_z(2 * step - 2)
                quantize_z(2 * step - 1)
            for ch in closing(step - 1):
                second_stage(ch)

        for q in range(4):
            engine = nc.sync if q % 2 == 0 else nc.scalar
            engine.dma_start(
                out=out_2[0, 4 * q : 4 * q + 4, :].bitcast(I32),
                in_=y_plane[32 * q : 32 * q + 4, :].bitcast(I32),
            )
